import numpy as np
import ml_dtypes


def mxq(x, axis, fmt="e4m3"):
    dtype, down = {"e4m3": (ml_dtypes.float8_e4m3fn, 7), "e5m2": (ml_dtypes.float8_e5m2, 14)}[fmt]
    v = np.moveaxis(np.asarray(x, np.float32).astype(ml_dtypes.bfloat16).astype(np.float64), axis, -1)
    blocks = v.reshape(v.shape[:-1] + (-1, 32))
    amax = np.abs(blocks).max(-1, keepdims=True)
    byte = np.maximum(np.where(amax > 0, np.frexp(amax)[1] - 1 + 127, 0) - down, 1)
    scale = np.exp2(byte - 127.0)
    codes = (blocks / scale).astype(np.float32).astype(dtype).astype(np.float64)
    return np.moveaxis((codes * scale).reshape(v.shape), -1, axis)


WIDE = False


def mx_kscale(k):
    if not WIDE:
        return np.ones(k)
    levels = np.array([10, -10, 5, -5, 0])
    if k % 512:
        return np.exp2(np.random.permutation(np.resize(levels, k // 32))).repeat(32)
    a = np.empty((k // 512, 16))
    for p in range(k // 512):
        a[p, :8] = np.random.permutation(np.resize(levels, 8))
        for g in range(8):
            far = levels[np.abs(levels - a[p, g]) >= 10]
            a[p, g + 8] = far[np.random.randint(len(far))]
    return np.exp2(a.ravel()).repeat(32)


def f64(x):
    return np.asarray(x).astype(np.float64)


def striped(idx):
    return np.tile(idx.reshape(-1, 16).T, (8, 1)).astype(np.uint16)


def unstriped(offs):
    return offs[:16].T.reshape(-1).astype(np.int64)


E2M1 = np.array([0.0, 0.5, 1.0, 1.5, 2.0, 3.0, 4.0, 6.0, -0.0, -0.5, -1.0, -1.5, -2.0, -3.0, -4.0, -6.0])


def pack_weight(w, fmt):
    k, n = w.shape
    w = f64(np.asarray(w, np.float32).astype(ml_dtypes.bfloat16)).reshape(k // 32, 32, n)
    amax = np.abs(w).max(1)
    if fmt == "e4m3":
        byte = np.frexp(amax)[1] - 1 + 127 - 7
    else:
        mant, ex = np.frexp(amax / 6.0)
        byte = np.where(mant > 0.5, ex, ex - 1) + 127
    byte = np.clip(np.where(amax > 0, byte, 1), 1, 254)
    scaled = (w * np.exp2(127.0 - byte)[:, None, :]).reshape(k, n).astype(np.float32)
    by_word = np.ascontiguousarray(scaled.reshape(k // 512, 128, 4, n).transpose(0, 1, 3, 2))
    if fmt == "e4m3":
        words = by_word.astype(ml_dtypes.float8_e4m3fn).view(np.uint8)
    else:
        c = by_word.astype(ml_dtypes.float4_e2m1fn).view(np.uint8) & 0xF
        words = (c[..., 0::2] | (c[..., 1::2] << 4)).reshape(k // 512, 128, 2 * n)
    return np.ascontiguousarray(words), np.ascontiguousarray(byte.astype(np.uint8).reshape(k // 512, 16, n))


def unpack_weight(words, scales, fmt):
    g, _, n = scales.shape
    words = np.ascontiguousarray(words).reshape(g, 128, n, -1)
    if fmt == "e4m3":
        vals = words.view(ml_dtypes.float8_e4m3fn).astype(np.float64)
    else:
        nib = np.empty((g, 128, n, 4), np.uint8)
        nib[..., 0::2] = words & 0xF
        nib[..., 1::2] = words >> 4
        vals = E2M1[nib]
    vals = vals * np.repeat(np.exp2(scales.astype(np.float64) - 127.0), 8, axis=1)[..., None]
    return vals.transpose(0, 1, 3, 2).reshape(g * 512, n)


def pack_table(v):
    words, scales = pack_weight(v, "e4m3")
    return np.concatenate([words.reshape(words.shape[0], -1), scales.reshape(scales.shape[0], -1)], axis=1)


def unpack_table(tab):
    g, t = tab.shape[0], tab.shape[1] // 528
    return unpack_weight(tab[:, :512 * t].reshape(g, 128, t, 4), tab[:, 512 * t:].reshape(g, 16, t), "e4m3")


G, K, M, T, S = 4, 1024, 512, 2048, 256


def setup_inputs():
    n = np.random.standard_normal
    s = mx_kscale(K)[:, None]
    return {
        "tab": pack_table(n((K, T)) * s),
        "w": (n((K, M)) / np.sqrt(K) / s).astype(np.float32),
        "b": (0.3 * n(512)).astype(np.float32),
        "offs": striped(np.concatenate([np.random.permutation(T)[:S] for _ in range(G)])),
    }


def reference(tab, w, b, offs):
    tab_ = unpack_table(tab)[:, unstriped(offs).reshape(G, S)].sum(1)
    w_ = mxq(f64(w), 0, "e4m3")
    y = w_.T @ tab_
    return y + f64(b)[:, None]

@@ -1,0 +1,126 @@
+from contextlib import ExitStack
+
+import concourse.mybir as mybir
+
+G, K, M, T, S = 4, 1024, 512, 2048, 256
+FLOPS = 2 * G * K * M * S
+
+F32 = mybir.dt.float32
+BF16 = mybir.dt.bfloat16
+I32 = mybir.dt.int32
+U32 = mybir.dt.uint32
+U16 = mybir.dt.uint16
+U8 = mybir.dt.uint8
+FP8X4 = mybir.dt.float8_e4m3fn_x4
+
+P = 128
+PACK = 4
+K_PASS = P * PACK
+HALF = M // 2
+LIST_COLS = S // 16
+
+
+def tile_list_tabbag_bias_kernel(tc, tab, w, b, offs, out):
+    nc = tc.nc
+    with ExitStack() as ctx:
+        sb = ctx.enter_context(tc.tile_pool(name="sb", bufs=1))
+        ps = ctx.enter_context(tc.psum_pool(name="ps", bufs=1))
+
+        offsets = sb.tile([P, G * LIST_COLS], U16, name="offsets")
+        nc.sync.dma_start(offsets[:], offs)
+        bias = sb.tile([P, M // P], F32, name="bias")
+        with nc.allow_non_contiguous_dma(reason="one bias value a partition"):
+            nc.sync.dma_start(bias[:], b.rearrange("(c p) -> p c", p=P))
+
+        tab_scales = sb.tile([P, T], U8, name="tab_scales", align_bytes=64)
+        nc.vector.memset(tab_scales[:].bitcast(I32), 0)
+
+        def load_w(a, lo, width):
+            raw = sb.tile([P, PACK, width], F32, name="w_raw_%d_%d" % (a, lo), align_bytes=64)
+            rows = w[a * K_PASS : (a + 1) * K_PASS, lo : lo + width]
+            nc.sync.dma_start(raw[:], rows.rearrange("(p j) n -> p j n", j=PACK))
+            return raw
+
+        def load_words(a):
+            words = sb.tile([P, T], I32, name="tab_words_%d" % a, align_bytes=64)
+            src = tab[a, 0 : K_PASS * T].rearrange("(p c) -> p c", p=P).bitcast(I32)
+            nc.sync.dma_start(words[:], src)
+            return words
+
+        for q in range(4):
+            lo = K_PASS * T + 4 * q * T
+            src = tab[:, lo : lo + 4 * T].rearrange("a (r t) -> a r t", r=4).bitcast(I32)
+            nc.sync.dma_start(tab_scales[32 * q : 32 * q + 8, :].bitcast(I32), src)
+        tab_words = [load_words(0)]
+        w_first = [load_w(0, h * HALF, HALF) for h in range(2)]
+        tab_words.append(load_words(1))
+        w_second = [load_w(1, n * P, P) for n in range(M // P)]
+
+        def round_w(raw, width, name):
+            grouped = sb.tile([P, width * PACK], BF16, name=name, align_bytes=64)
+            nc.scalar.copy(
+                grouped[:].rearrange("p (c i t) -> p c t i", i=4, t=PACK),
+                raw[:].rearrange("p t (c i) -> p c t i", i=4),
+            )
+            return grouped
+
+        def quantise(grouped, width, name):
+            codes = sb.tile([P, width], U32, name="w_codes_" + name, align_bytes=64)
+            scales = sb.tile([P, width], U8, name="w_scales_" + name, align_bytes=64)
+            nc.vector.quantize_mx(out=codes[:].bitcast(FP8X4), scales=scales[:], in_=grouped[:])
+            return codes, scales
+
+        def gather_words(a, g, tag):
+            picked = sb.tile([P, S], U32, name="picked_%d_%d" % (a, g), tag=tag, align_bytes=64)
+            window = tab_words[a][:].bitcast(U32)
+            nc.vector.tensor_copy(picked[:], window.indirect(offsets[:, g * LIST_COLS : (g + 1) * LIST_COLS]))
+            return picked
+
+        picked_scales = sb.tile([P, G * S], U8, name="picked_scales", align_bytes=64)
+        nc.vector.tensor_copy(picked_scales[:], tab_scales[:].indirect(offsets[:]))
+
+        acc = [ps.tile([P, S], F32, name="acc_%d" % n) for n in range(M // P)]
+
+        def multiply(a, g, n, picked, quantised, lo):
+            codes, scales = quantised
+            nc.tensor.matmul_mx(
+                out=acc[n][:],
+                lhsT=codes[:, lo : lo + P].bitcast(FP8X4),
+                lhsT_scale=scales[:, lo : lo + P],
+                rhs=picked[:].bitcast(FP8X4),
+                rhs_scale=picked_scales[4 * a : P, g * S : (g + 1) * S],
+                start=(a == 0 and g == 0),
+                stop=(a == 1 and g == G - 1),
+            )
+
+        picked = [gather_words(0, g, "picked_0_%d" % g) for g in range(G)]
+        for h in range(2):
+            quantised = quantise(round_w(w_first[h], HALF, "w_bf_0_%d" % h), HALF, "0_%d" % h)
+            for n in range(2):
+                for g in range(G):
+                    multiply(0, g, 2 * h + n, picked[g], quantised, n * P)
+
+        grouped = [round_w(w_second[n], P, "w_bf_1_%d" % n) for n in range(M // P)]
+        picked = [gather_words(1, g, "picked_1_%d" % g) for g in range(2)]
+        quantised = [quantise(grouped[0], P, "1_0")]
+        picked.append(gather_words(1, 2, "w_bf_1_0"))
+        for g in range(3):
+            multiply(1, g, 0, picked[g], quantised[0], 0)
+        quantised.append(quantise(grouped[1], P, "1_1"))
+        picked.append(gather_words(1, 3, "w_bf_1_1"))
+        for g in range(3):
+            multiply(1, g, 1, picked[g], quantised[1], 0)
+        for n in range(2):
+            multiply(1, 3, n, picked[3], quantised[n], 0)
+        for n in range(2, 4):
+            quantised.append(quantise(grouped[n], P, "1_%d" % n))
+        early = sb.tile([P, 2, S], F32, name="early", tag="w_raw_1_%d" % (3 * P), align_bytes=64)
+        for n in range(2):
+            nc.scalar.activation(early[:, n, :], acc[n][:], mybir.ActivationFunctionType.Identity, bias=bias[:, n : n + 1])
+            nc.sync.dma_start(out[n * P : (n + 1) * P, :], early[:, n, :])
+        for n in range(2, 4):
+            for g in range(G):
+                multiply(1, g, n, picked[g], quantised[n], 0)
+            result = sb.tile([P, S], F32, name="result_%d" % n)
+            nc.vector.tensor_scalar(result[:], acc[n][:], bias[:, n : n + 1], None, mybir.AluOpType.add)
+            nc.sync.dma_start(out[n * P : (n + 1) * P, :], result[:])

@@ -1,6 +1,7 @@
 from contextlib import ExitStack
 
 import concourse.mybir as mybir
+from concourse.masks import make_identity
 
 G, K, M, T, S = 4, 1024, 512, 2048, 256
 FLOPS = 2 * G * K * M * S
@@ -28,9 +29,15 @@ def tile_list_tabbag_bias_kernel(tc, tab, w, b, offs, out):
 
         offsets = sb.tile([P, G * LIST_COLS], U16, name="offsets")
         nc.sync.dma_start(offsets[:], offs)
+        bias_rows = sb.tile([P, P], F32, name="bias_rows")
+        nc.gpsimd.memset(bias_rows[:], 0.0)
+        nc.sync.dma_start(bias_rows[0 : M // P, :], b.rearrange("(c p) -> c p", p=P))
+        identity = sb.tile([P, P], F32, name="identity")
+        make_identity(nc, identity[:])
+        bias_turned = ps.tile([P, P], F32, name="bias_turned")
+        nc.tensor.transpose(bias_turned[:], bias_rows[:], identity[:])
         bias = sb.tile([P, M // P], F32, name="bias")
-        with nc.allow_non_contiguous_dma(reason="one bias value a partition"):
-            nc.sync.dma_start(bias[:], b.rearrange("(c p) -> p c", p=P))
+        nc.scalar.copy(bias[:], bias_turned[:, 0 : M // P])
 
         tab_scales = sb.tile([P, T], U8, name="tab_scales", align_bytes=64)
         nc.vector.memset(tab_scales[:].bitcast(I32), 0)

@@ -1,7 +1,6 @@
 from contextlib import ExitStack
 
 import concourse.mybir as mybir
-from concourse.masks import make_identity
 
 G, K, M, T, S = 4, 1024, 512, 2048, 256
 FLOPS = 2 * G * K * M * S
@@ -29,15 +28,6 @@ def tile_list_tabbag_bias_kernel(tc, tab, w, b, offs, out):
 
         offsets = sb.tile([P, G * LIST_COLS], U16, name="offsets")
         nc.sync.dma_start(offsets[:], offs)
-        bias_rows = sb.tile([P, P], F32, name="bias_rows")
-        nc.gpsimd.memset(bias_rows[:], 0.0)
-        nc.sync.dma_start(bias_rows[0 : M // P, :], b.rearrange("(c p) -> c p", p=P))
-        identity = sb.tile([P, P], F32, name="identity")
-        make_identity(nc, identity[:])
-        bias_turned = ps.tile([P, P], F32, name="bias_turned")
-        nc.tensor.transpose(bias_turned[:], bias_rows[:], identity[:])
-        bias = sb.tile([P, M // P], F32, name="bias")
-        nc.scalar.copy(bias[:], bias_turned[:, 0 : M // P])
 
         tab_scales = sb.tile([P, T], U8, name="tab_scales", align_bytes=64)
         nc.vector.memset(tab_scales[:].bitcast(I32), 0)
@@ -54,14 +44,18 @@ def tile_list_tabbag_bias_kernel(tc, tab, w, b, offs, out):
             nc.sync.dma_start(words[:], src)
             return words
 
+        w_first = [load_w(0, 0, HALF)]
         for q in range(4):
             lo = K_PASS * T + 4 * q * T
             src = tab[:, lo : lo + 4 * T].rearrange("a (r t) -> a r t", r=4).bitcast(I32)
             nc.sync.dma_start(tab_scales[32 * q : 32 * q + 8, :].bitcast(I32), src)
         tab_words = [load_words(0)]
-        w_first = [load_w(0, h * HALF, HALF) for h in range(2)]
+        w_first.append(load_w(0, HALF, HALF))
         tab_words.append(load_words(1))
         w_second = [load_w(1, n * P, P) for n in range(M // P)]
+        bias = sb.tile([P, M // P], F32, name="bias")
+        with nc.allow_non_contiguous_dma(reason="one bias value a partition"):
+            nc.sync.dma_start(bias[:], b.rearrange("(c p) -> p c", p=P))
 
         def round_w(raw, width, name):
             grouped = sb.tile([P, width * PACK], BF16, name=name, align_bytes=64)
@@ -100,12 +94,16 @@ def tile_list_tabbag_bias_kernel(tc, tab, w, b, offs, out):
                 stop=(a == 1 and g == G - 1),
             )
 
-        picked = [gather_words(0, g, "picked_0_%d" % g) for g in range(G)]
-        for h in range(2):
-            quantised = quantise(round_w(w_first[h], HALF, "w_bf_0_%d" % h), HALF, "0_%d" % h)
+        quantised = quantise(round_w(w_first[0], HALF, "w_bf_0_0"), HALF, "0_0")
+        picked = []
+        for g in range(G):
+            picked.append(gather_words(0, g, "picked_0_%d" % g))
             for n in range(2):
-                for g in range(G):
-                    multiply(0, g, 2 * h + n, picked[g], quantised, n * P)
+                multiply(0, g, n, picked[g], quantised, n * P)
+        quantised = quantise(round_w(w_first[1], HALF, "w_bf_0_1"), HALF, "0_1")
+        for n in range(2):
+            for g in range(G):
+                multiply(0, g, 2 + n, picked[g], quantised, n * P)
 
         grouped = [round_w(w_second[n], P, "w_bf_1_%d" % n) for n in range(M // P)]
         picked = [gather_words(1, g, "picked_1_%d" % g) for g in range(2)]

@@ -44,11 +44,12 @@ def tile_list_tabbag_bias_kernel(tc, tab, w, b, offs, out):
             nc.sync.dma_start(words[:], src)
             return words
 
-        w_first = [load_w(0, 0, HALF)]
+        w_first = [load_w(0, 0, P)]
         for q in range(4):
             lo = K_PASS * T + 4 * q * T
             src = tab[:, lo : lo + 4 * T].rearrange("a (r t) -> a r t", r=4).bitcast(I32)
             nc.sync.dma_start(tab_scales[32 * q : 32 * q + 8, :].bitcast(I32), src)
+        w_first.append(load_w(0, P, P))
         tab_words = [load_words(0)]
         w_first.append(load_w(0, HALF, HALF))
         tab_words.append(load_words(1))
@@ -57,12 +58,13 @@ def tile_list_tabbag_bias_kernel(tc, tab, w, b, offs, out):
         with nc.allow_non_contiguous_dma(reason="one bias value a partition"):
             nc.sync.dma_start(bias[:], b.rearrange("(c p) -> p c", p=P))
 
-        def round_w(raw, width, name):
-            grouped = sb.tile([P, width * PACK], BF16, name=name, align_bytes=64)
-            nc.scalar.copy(
-                grouped[:].rearrange("p (c i t) -> p c t i", i=4, t=PACK),
-                raw[:].rearrange("p t (c i) -> p c t i", i=4),
-            )
+        def round_w(raws, width, name):
+            grouped = sb.tile([P, len(raws) * width * PACK], BF16, name=name, align_bytes=64)
+            for u, raw in enumerate(raws):
+                nc.scalar.copy(
+                    grouped[:, u * width * PACK : (u + 1) * width * PACK].rearrange("p (c i t) -> p c t i", i=4, t=PACK),
+                    raw[:].rearrange("p t (c i) -> p c t i", i=4),
+                )
             return grouped
 
         def quantise(grouped, width, name):
@@ -94,25 +96,25 @@ def tile_list_tabbag_bias_kernel(tc, tab, w, b, offs, out):
                 stop=(a == 1 and g == G - 1),
             )
 
-        quantised = quantise(round_w(w_first[0], HALF, "w_bf_0_0"), HALF, "0_0")
+        quantised = quantise(round_w(w_first[0:2], P, "w_bf_0_0"), HALF, "0_0")
         picked = []
         for g in range(G):
             picked.append(gather_words(0, g, "picked_0_%d" % g))
             for n in range(2):
                 multiply(0, g, n, picked[g], quantised, n * P)
-        quantised = quantise(round_w(w_first[1], HALF, "w_bf_0_1"), HALF, "0_1")
+        quantised = quantise(round_w(w_first[2:3], HALF, "w_bf_0_1"), HALF, "0_1")
         for n in range(2):
             for g in range(G):
                 multiply(0, g, 2 + n, picked[g], quantised, n * P)
 
-        grouped = [round_w(w_second[n], P, "w_bf_1_%d" % n) for n in range(M // P)]
+        grouped = [round_w(w_second[n : n + 1], P, "w_bf_1_%d" % n) for n in range(M // P)]
         picked = [gather_words(1, g, "picked_1_%d" % g) for g in range(2)]
         quantised = [quantise(grouped[0], P, "1_0")]
-        picked.append(gather_words(1, 2, "w_bf_1_0"))
+        picked.append(gather_words(1, 2, "w_raw_1_0"))
         for g in range(3):
             multiply(1, g, 0, picked[g], quantised[0], 0)
         quantised.append(quantise(grouped[1], P, "1_1"))
-        picked.append(gather_words(1, 3, "w_bf_1_1"))
+        picked.append(gather_words(1, 3, "w_raw_1_%d" % P))
         for g in range(3):
             multiply(1, g, 1, picked[g], quantised[1], 0)
         for n in range(2):

@@ -27,7 +27,6 @@ def tile_list_tabbag_bias_kernel(tc, tab, w, b, offs, out):
         ps = ctx.enter_context(tc.psum_pool(name="ps", bufs=1))
 
         offsets = sb.tile([P, G * LIST_COLS], U16, name="offsets")
-        nc.sync.dma_start(offsets[:], offs)
 
         tab_scales = sb.tile([P, T], U8, name="tab_scales", align_bytes=64)
         nc.vector.memset(tab_scales[:].bitcast(I32), 0)
@@ -45,6 +44,7 @@ def tile_list_tabbag_bias_kernel(tc, tab, w, b, offs, out):
             return words
 
         w_first = [load_w(0, 0, P)]
+        nc.sync.dma_start(offsets[:], offs)
         for q in range(4):
             lo = K_PASS * T + 4 * q * T
             src = tab[:, lo : lo + 4 * T].rearrange("a (r t) -> a r t", r=4).bitcast(I32)
@@ -82,16 +82,18 @@ def tile_list_tabbag_bias_kernel(tc, tab, w, b, offs, out):
         picked_scales = sb.tile([P, G * S], U8, name="picked_scales", align_bytes=64)
         nc.vector.tensor_copy(picked_scales[:], tab_scales[:].indirect(offsets[:]))
 
-        acc = [ps.tile([P, S], F32, name="acc_%d" % n) for n in range(M // P)]
+        acc = [[ps.tile([P, S], F32, name="acc_%d" % n)] for n in range(3)]
+        acc.append([ps.tile([P, S // 2], F32, name="acc_3_%d" % h) for h in range(2)])
 
-        def multiply(a, g, n, picked, quantised, lo):
+        def multiply(a, g, n, picked, quantised, lo, part=0):
             codes, scales = quantised
+            width = S // len(acc[n])
             nc.tensor.matmul_mx(
-                out=acc[n][:],
+                out=acc[n][part][:],
                 lhsT=codes[:, lo : lo + P].bitcast(FP8X4),
                 lhsT_scale=scales[:, lo : lo + P],
-                rhs=picked[:].bitcast(FP8X4),
-                rhs_scale=picked_scales[4 * a : P, g * S : (g + 1) * S],
+                rhs=picked[:, part * width : (part + 1) * width].bitcast(FP8X4),
+                rhs_scale=picked_scales[4 * a : P, g * S + part * width : g * S + (part + 1) * width],
                 start=(a == 0 and g == 0),
                 stop=(a == 1 and g == G - 1),
             )
@@ -104,8 +106,9 @@ def tile_list_tabbag_bias_kernel(tc, tab, w, b, offs, out):
                 multiply(0, g, n, picked[g], quantised, n * P)
         quantised = quantise(round_w(w_first[2:3], HALF, "w_bf_0_1"), HALF, "0_1")
         for n in range(2):
-            for g in range(G):
-                multiply(0, g, 2 + n, picked[g], quantised, n * P)
+            for part in range(len(acc[2 + n])):
+                for g in range(G):
+                    multiply(0, g, 2 + n, picked[g], quantised, n * P, part)
 
         grouped = [round_w(w_second[n : n + 1], P, "w_bf_1_%d" % n) for n in range(M // P)]
         picked = [gather_words(1, g, "picked_1_%d" % g) for g in range(2)]
@@ -123,11 +126,19 @@ def tile_list_tabbag_bias_kernel(tc, tab, w, b, offs, out):
             quantised.append(quantise(grouped[n], P, "1_%d" % n))
         early = sb.tile([P, 2, S], F32, name="early", tag="w_raw_1_%d" % (3 * P), align_bytes=64)
         for n in range(2):
-            nc.scalar.activation(early[:, n, :], acc[n][:], mybir.ActivationFunctionType.Identity, bias=bias[:, n : n + 1])
+            nc.scalar.activation(early[:, n, :], acc[n][0][:], mybir.ActivationFunctionType.Identity, bias=bias[:, n : n + 1])
             nc.sync.dma_start(out[n * P : (n + 1) * P, :], early[:, n, :])
-        for n in range(2, 4):
+        for g in range(G):
+            multiply(1, g, 2, picked[g], quantised[2], 0)
+        result = sb.tile([P, S], F32, name="result_2")
+        nc.vector.tensor_scalar(result[:], acc[2][0][:], bias[:, 2:3], None, mybir.AluOpType.add)
+        nc.sync.dma_start(out[2 * P : 3 * P, :], result[:])
+        for part in range(2):
             for g in range(G):
-                multiply(1, g, n, picked[g], quantised[n], 0)
-            result = sb.tile([P, S], F32, name="result_%d" % n)
-            nc.vector.tensor_scalar(result[:], acc[n][:], bias[:, n : n + 1], None, mybir.AluOpType.add)
-            nc.sync.dma_start(out[n * P : (n + 1) * P, :], result[:])
+                multiply(1, g, 3, picked[g], quantised[3], 0, part)
+            result = sb.tile([P, S // 2], F32, name="result_3_%d" % part)
+            if part == 0:
+                nc.scalar.activation(result[:], acc[3][0][:], mybir.ActivationFunctionType.Identity, bias=bias[:, 3:4])
+            else:
+                nc.vector.tensor_scalar(result[:], acc[3][1][:], bias[:, 3:4], None, mybir.AluOpType.add)
+            nc.sync.dma_start(out[3 * P : 4 * P, part * (S // 2) : (part + 1) * (S // 2)], result[:])

@@ -49,9 +49,8 @@ def tile_list_tabbag_bias_kernel(tc, tab, w, b, offs, out):
             lo = K_PASS * T + 4 * q * T
             src = tab[:, lo : lo + 4 * T].rearrange("a (r t) -> a r t", r=4).bitcast(I32)
             nc.sync.dma_start(tab_scales[32 * q : 32 * q + 8, :].bitcast(I32), src)
-        w_first.append(load_w(0, P, P))
         tab_words = [load_words(0)]
-        w_first.append(load_w(0, HALF, HALF))
+        w_first.append(load_w(0, P, M - P))
         tab_words.append(load_words(1))
         w_second = [load_w(1, n * P, P) for n in range(M // P)]
         bias = sb.tile([P, M // P], F32, name="bias")
@@ -63,7 +62,7 @@ def tile_list_tabbag_bias_kernel(tc, tab, w, b, offs, out):
             for u, raw in enumerate(raws):
                 nc.scalar.copy(
                     grouped[:, u * width * PACK : (u + 1) * width * PACK].rearrange("p (c i t) -> p c t i", i=4, t=PACK),
-                    raw[:].rearrange("p t (c i) -> p c t i", i=4),
+                    raw.rearrange("p t (c i) -> p c t i", i=4),
                 )
             return grouped
 
@@ -98,19 +97,21 @@ def tile_list_tabbag_bias_kernel(tc, tab, w, b, offs, out):
                 stop=(a == 1 and g == G - 1),
             )
 
-        quantised = quantise(round_w(w_first[0:2], P, "w_bf_0_0"), HALF, "0_0")
+        quantised = quantise(round_w([w_first[0][:]], P, "w_bf_0_0"), P, "0_0")
         picked = []
         for g in range(G):
             picked.append(gather_words(0, g, "picked_0_%d" % g))
-            for n in range(2):
-                multiply(0, g, n, picked[g], quantised, n * P)
-        quantised = quantise(round_w(w_first[2:3], HALF, "w_bf_0_1"), HALF, "0_1")
+            multiply(0, g, 0, picked[g], quantised, 0)
+        quantised = quantise(round_w([w_first[1][:, :, 0:P]], P, "w_bf_0_1"), P, "0_1")
+        for g in range(G):
+            multiply(0, g, 1, picked[g], quantised, 0)
+        quantised = quantise(round_w([w_first[1][:, :, P : M - P]], HALF, "w_bf_0_2"), HALF, "0_2")
         for n in range(2):
             for part in range(len(acc[2 + n])):
                 for g in range(G):
                     multiply(0, g, 2 + n, picked[g], quantised, n * P, part)
 
-        grouped = [round_w(w_second[n : n + 1], P, "w_bf_1_%d" % n) for n in range(M // P)]
+        grouped = [round_w([w_second[n][:]], P, "w_bf_1_%d" % n) for n in range(M // P)]
         picked = [gather_words(1, g, "picked_1_%d" % g) for g in range(2)]
         quantised = [quantise(grouped[0], P, "1_0")]
         picked.append(gather_words(1, 2, "w_raw_1_0"))

@@ -31,11 +31,11 @@ def tile_list_tabbag_bias_kernel(tc, tab, w, b, offs, out):
         tab_scales = sb.tile([P, T], U8, name="tab_scales", align_bytes=64)
         nc.vector.memset(tab_scales[:].bitcast(I32), 0)
 
-        def load_w(a, lo, width):
-            raw = sb.tile([P, PACK, width], F32, name="w_raw_%d_%d" % (a, lo), align_bytes=64)
-            rows = w[a * K_PASS : (a + 1) * K_PASS, lo : lo + width]
+        def load_w(a, n, tiles):
+            raw = sb.tile([P, PACK, tiles * P], F32, name="w_raw_%d_%d" % (a, n), align_bytes=64)
+            rows = w[a * K_PASS : (a + 1) * K_PASS, n * P : (n + tiles) * P]
             nc.sync.dma_start(raw[:], rows.rearrange("(p j) n -> p j n", j=PACK))
-            return raw
+            return [raw[:, :, u * P : (u + 1) * P] for u in range(tiles)]
 
         def load_words(a):
             words = sb.tile([P, T], I32, name="tab_words_%d" % a, align_bytes=64)
@@ -43,103 +43,105 @@ def tile_list_tabbag_bias_kernel(tc, tab, w, b, offs, out):
             nc.sync.dma_start(words[:], src)
             return words
 
-        w_first = [load_w(0, 0, P)]
+        def load_scales():
+            for q in range(4):
+                lo = K_PASS * T + 4 * q * T
+                src = tab[:, lo : lo + 4 * T].rearrange("a (r t) -> a r t", r=4).bitcast(I32)
+                nc.sync.dma_start(tab_scales[32 * q : 32 * q + 8, :].bitcast(I32), src)
+
+        w_raw = [load_w(0, 0, 1), []]
         nc.sync.dma_start(offsets[:], offs)
-        for q in range(4):
-            lo = K_PASS * T + 4 * q * T
-            src = tab[:, lo : lo + 4 * T].rearrange("a (r t) -> a r t", r=4).bitcast(I32)
-            nc.sync.dma_start(tab_scales[32 * q : 32 * q + 8, :].bitcast(I32), src)
+        load_scales()
         tab_words = [load_words(0)]
-        w_first.append(load_w(0, P, M - P))
+        w_raw[0].extend(load_w(0, 1, 2))
         tab_words.append(load_words(1))
-        w_second = [load_w(1, n * P, P) for n in range(M // P)]
+        w_raw[0].extend(load_w(0, 3, 1))
+        for n in range(M // P):
+            w_raw[1].extend(load_w(1, n, 1))
         bias = sb.tile([P, M // P], F32, name="bias")
         with nc.allow_non_contiguous_dma(reason="one bias value a partition"):
             nc.sync.dma_start(bias[:], b.rearrange("(c p) -> p c", p=P))
 
-        def round_w(raws, width, name):
-            grouped = sb.tile([P, len(raws) * width * PACK], BF16, name=name, align_bytes=64)
-            for u, raw in enumerate(raws):
-                nc.scalar.copy(
-                    grouped[:, u * width * PACK : (u + 1) * width * PACK].rearrange("p (c i t) -> p c t i", i=4, t=PACK),
-                    raw.rearrange("p t (c i) -> p c t i", i=4),
-                )
+        def round_w(a, n):
+            grouped = sb.tile([P, P * PACK], BF16, name="w_bf_%d_%d" % (a, n), align_bytes=64)
+            nc.scalar.copy(
+                grouped[:].rearrange("p (c i t) -> p c t i", i=4, t=PACK),
+                w_raw[a][n].rearrange("p t (c i) -> p c t i", i=4),
+            )
             return grouped
 
-        def quantise(grouped, width, name):
-            codes = sb.tile([P, width], U32, name="w_codes_" + name, align_bytes=64)
-            scales = sb.tile([P, width], U8, name="w_scales_" + name, align_bytes=64)
-            nc.vector.quantize_mx(out=codes[:].bitcast(FP8X4), scales=scales[:], in_=grouped[:])
-            return codes, scales
+        def quantise(a, n):
+            codes = sb.tile([P, P], U32, name="w_codes_%d_%d" % (a, n), align_bytes=64)
+            scales = sb.tile([P, P], U8, name="w_scales_%d_%d" % (a, n), align_bytes=64)
+            nc.vector.quantize_mx(out=codes[:].bitcast(FP8X4), scales=scales[:], in_=grouped[a][n][:])
+            quantised[a, n] = (codes, scales)
 
-        def gather_words(a, g, tag):
-            picked = sb.tile([P, S], U32, name="picked_%d_%d" % (a, g), tag=tag, align_bytes=64)
+        def gather_words(a, g, bags, tag):
+            tile = sb.tile([P, bags * S], U32, name="picked_%d_%d" % (a, g), tag=tag, align_bytes=64)
             window = tab_words[a][:].bitcast(U32)
-            nc.vector.tensor_copy(picked[:], window.indirect(offsets[:, g * LIST_COLS : (g + 1) * LIST_COLS]))
-            return picked
+            nc.vector.tensor_copy(tile[:], window.indirect(offsets[:, g * LIST_COLS : (g + bags) * LIST_COLS]))
+            for u in range(bags):
+                picked[a, g + u] = tile[:, u * S : (u + 1) * S]
+
+        def multiply(a, n, bags, part=0):
+            codes, scales = quantised[a, n]
+            width = S // len(acc[n])
+            for g in bags:
+                nc.tensor.matmul_mx(
+                    out=acc[n][part][:],
+                    lhsT=codes[:].bitcast(FP8X4),
+                    lhsT_scale=scales[:],
+                    rhs=picked[a, g][:, part * width : (part + 1) * width].bitcast(FP8X4),
+                    rhs_scale=picked_scales[4 * a : P, g * S + part * width : g * S + (part + 1) * width],
+                    start=(a == 0 and g == 0),
+                    stop=(a == 1 and g == G - 1),
+                )
+
+        def finish_on_scalar(result, n, part=0):
+            nc.scalar.activation(result, acc[n][part][:], mybir.ActivationFunctionType.Identity, bias=bias[:, n : n + 1])
+
+        def finish_on_vector(result, n, part=0):
+            nc.vector.tensor_scalar(result, acc[n][part][:], bias[:, n : n + 1], None, mybir.AluOpType.add)
 
         picked_scales = sb.tile([P, G * S], U8, name="picked_scales", align_bytes=64)
         nc.vector.tensor_copy(picked_scales[:], tab_scales[:].indirect(offsets[:]))
 
+        quantised = {}
+        picked = {}
         acc = [[ps.tile([P, S], F32, name="acc_%d" % n)] for n in range(3)]
         acc.append([ps.tile([P, S // 2], F32, name="acc_3_%d" % h) for h in range(2)])
+        grouped = [[round_w(a, n) for n in range(M // P)] for a in range(2)]
 
-        def multiply(a, g, n, picked, quantised, lo, part=0):
-            codes, scales = quantised
-            width = S // len(acc[n])
-            nc.tensor.matmul_mx(
-                out=acc[n][part][:],
-                lhsT=codes[:, lo : lo + P].bitcast(FP8X4),
-                lhsT_scale=scales[:, lo : lo + P],
-                rhs=picked[:, part * width : (part + 1) * width].bitcast(FP8X4),
-                rhs_scale=picked_scales[4 * a : P, g * S + part * width : g * S + (part + 1) * width],
-                start=(a == 0 and g == 0),
-                stop=(a == 1 and g == G - 1),
-            )
-
-        quantised = quantise(round_w([w_first[0][:]], P, "w_bf_0_0"), P, "0_0")
-        picked = []
-        for g in range(G):
-            picked.append(gather_words(0, g, "picked_0_%d" % g))
-            multiply(0, g, 0, picked[g], quantised, 0)
-        quantised = quantise(round_w([w_first[1][:, :, 0:P]], P, "w_bf_0_1"), P, "0_1")
-        for g in range(G):
-            multiply(0, g, 1, picked[g], quantised, 0)
-        quantised = quantise(round_w([w_first[1][:, :, P : M - P]], HALF, "w_bf_0_2"), HALF, "0_2")
-        for n in range(2):
-            for part in range(len(acc[2 + n])):
-                for g in range(G):
-                    multiply(0, g, 2 + n, picked[g], quantised, n * P, part)
-
-        grouped = [round_w([w_second[n][:]], P, "w_bf_1_%d" % n) for n in range(M // P)]
-        picked = [gather_words(1, g, "picked_1_%d" % g) for g in range(2)]
-        quantised = [quantise(grouped[0], P, "1_0")]
-        picked.append(gather_words(1, 2, "w_raw_1_0"))
-        for g in range(3):
-            multiply(1, g, 0, picked[g], quantised[0], 0)
-        quantised.append(quantise(grouped[1], P, "1_1"))
-        picked.append(gather_words(1, 3, "w_raw_1_%d" % P))
-        for g in range(3):
-            multiply(1, g, 1, picked[g], quantised[1], 0)
-        for n in range(2):
-            multiply(1, 3, n, picked[3], quantised[n], 0)
-        for n in range(2, 4):
-            quantised.append(quantise(grouped[n], P, "1_%d" % n))
-        early = sb.tile([P, 2, S], F32, name="early", tag="w_raw_1_%d" % (3 * P), align_bytes=64)
-        for n in range(2):
-            nc.scalar.activation(early[:, n, :], acc[n][0][:], mybir.ActivationFunctionType.Identity, bias=bias[:, n : n + 1])
-            nc.sync.dma_start(out[n * P : (n + 1) * P, :], early[:, n, :])
-        for g in range(G):
-            multiply(1, g, 2, picked[g], quantised[2], 0)
-        result = sb.tile([P, S], F32, name="result_2")
-        nc.vector.tensor_scalar(result[:], acc[2][0][:], bias[:, 2:3], None, mybir.AluOpType.add)
-        nc.sync.dma_start(out[2 * P : 3 * P, :], result[:])
+        quantise(0, 0)
+        for g in (0, 2):
+            gather_words(0, g, 2, "picked_0_%d" % g)
+            multiply(0, 0, (g, g + 1))
+        for n in (1, 2):
+            quantise(0, n)
+            multiply(0, n, range(G))
+        gather_words(1, 0, 2, "picked_1_0")
+        quantise(0, 3)
         for part in range(2):
-            for g in range(G):
-                multiply(1, g, 3, picked[g], quantised[3], 0, part)
+            multiply(0, 3, range(G), part)
+        gather_words(1, 2, 1, "w_raw_0_3")
+        for n in range(2):
+            quantise(1, n)
+            multiply(1, n, range(3))
+        gather_words(1, 3, 1, "w_raw_1_1")
+        for n in range(2):
+            multiply(1, n, [3])
+        for n in (2, 3):
+            quantise(1, n)
+        early = sb.tile([P, 2, S], F32, name="early", tag="w_raw_1_3", align_bytes=64)
+        for n in range(2):
+            finish_on_scalar(early[:, n, :], n)
+            nc.sync.dma_start(out[n * P : (n + 1) * P, :], early[:, n, :])
+        multiply(1, 2, range(G))
+        result = sb.tile([P, S], F32, name="result_2")
+        finish_on_vector(result[:], 2)
+        nc.sync.dma_start(out[2 * P : 3 * P, :], result[:])
+        for part, finish in enumerate((finish_on_scalar, finish_on_vector)):
+            multiply(1, 3, range(G), part)
             result = sb.tile([P, S // 2], F32, name="result_3_%d" % part)
-            if part == 0:
-                nc.scalar.activation(result[:], acc[3][0][:], mybir.ActivationFunctionType.Identity, bias=bias[:, 3:4])
-            else:
-                nc.vector.tensor_scalar(result[:], acc[3][1][:], bias[:, 3:4], None, mybir.AluOpType.add)
+            finish(result[:], 3, part)
             nc.sync.dma_start(out[3 * P : 4 * P, part * (S // 2) : (part + 1) * (S // 2)], result[:])

@@ -62,9 +62,9 @@ def tile_list_tabbag_bias_kernel(tc, tab, w, b, offs, out):
         with nc.allow_non_contiguous_dma(reason="one bias value a partition"):
             nc.sync.dma_start(bias[:], b.rearrange("(c p) -> p c", p=P))
 
-        def round_w(a, n):
+        def round_w(a, n, copy):
             grouped = sb.tile([P, P * PACK], BF16, name="w_bf_%d_%d" % (a, n), align_bytes=64)
-            nc.scalar.copy(
+            copy(
                 grouped[:].rearrange("p (c i t) -> p c t i", i=4, t=PACK),
                 w_raw[a][n].rearrange("p t (c i) -> p c t i", i=4),
             )
@@ -110,7 +110,7 @@ def tile_list_tabbag_bias_kernel(tc, tab, w, b, offs, out):
         picked = {}
         acc = [[ps.tile([P, S], F32, name="acc_%d" % n)] for n in range(3)]
         acc.append([ps.tile([P, S // 2], F32, name="acc_3_%d" % h) for h in range(2)])
-        grouped = [[round_w(a, n) for n in range(M // P)] for a in range(2)]
+        grouped = [[round_w(a, n, nc.scalar.copy) for n in range(M // P - a)] for a in range(2)]
 
         quantise(0, 0)
         for g in (0, 2):
@@ -130,9 +130,10 @@ def tile_list_tabbag_bias_kernel(tc, tab, w, b, offs, out):
         gather_words(1, 3, 1, "w_raw_1_1")
         for n in range(2):
             multiply(1, n, [3])
-        for n in (2, 3):
-            quantise(1, n)
-        early = sb.tile([P, 2, S], F32, name="early", tag="w_raw_1_3", align_bytes=64)
+        quantise(1, 2)
+        grouped[1].append(round_w(1, 3, nc.vector.tensor_copy))
+        quantise(1, 3)
+        early = sb.tile([P, 2, S], F32, name="early", align_bytes=64)
         for n in range(2):
             finish_on_scalar(early[:, n, :], n)
             nc.sync.dma_start(out[n * P : (n + 1) * P, :], early[:, n, :])

@@ -44,10 +44,14 @@ def tile_list_tabbag_bias_kernel(tc, tab, w, b, offs, out):
             return words
 
         def load_scales():
-            for q in range(4):
+            for q in range(3):
                 lo = K_PASS * T + 4 * q * T
                 src = tab[:, lo : lo + 4 * T].rearrange("a (r t) -> a r t", r=4).bitcast(I32)
                 nc.sync.dma_start(tab_scales[32 * q : 32 * q + 8, :].bitcast(I32), src)
+            for a in range(2):
+                lo = K_PASS * T + 12 * T
+                src = tab[a, lo : lo + 4 * T].rearrange("(r t) -> r t", r=4).bitcast(I32)
+                nc.sync.dma_start(tab_scales[96 + 4 * a : 100 + 4 * a, :].bitcast(I32), src)
 
         w_raw = [load_w(0, 0, 1), []]
         nc.sync.dma_start(offsets[:], offs)

@@ -44,17 +44,19 @@ def tile_list_tabbag_bias_kernel(tc, tab, w, b, offs, out):
             return words
 
         def load_scales():
-            for q in range(3):
+            for q in (1, 3):
                 lo = K_PASS * T + 4 * q * T
                 src = tab[:, lo : lo + 4 * T].rearrange("a (r t) -> a r t", r=4).bitcast(I32)
-                nc.sync.dma_start(tab_scales[32 * q : 32 * q + 8, :].bitcast(I32), src)
-            for a in range(2):
-                lo = K_PASS * T + 12 * T
-                src = tab[a, lo : lo + 4 * T].rearrange("(r t) -> r t", r=4).bitcast(I32)
-                nc.sync.dma_start(tab_scales[96 + 4 * a : 100 + 4 * a, :].bitcast(I32), src)
+                nc.scalar.dma_start(tab_scales[32 * q : 32 * q + 8, :].bitcast(I32), src)
+            for q in (2, 0):
+                for a in range(2):
+                    lo = K_PASS * T + 4 * q * T
+                    src = tab[a, lo : lo + 4 * T].rearrange("(r t) -> r t", r=4).bitcast(I32)
+                    first = 32 * q + 4 * a
+                    nc.sync.dma_start(tab_scales[first : first + 4, :].bitcast(I32), src)
 
-        w_raw = [load_w(0, 0, 1), []]
         nc.sync.dma_start(offsets[:], offs)
+        w_raw = [load_w(0, 0, 1), []]
         load_scales()
         tab_words = [load_words(0)]
         w_raw[0].extend(load_w(0, 1, 2))

@@ -68,12 +68,14 @@ def tile_list_tabbag_bias_kernel(tc, tab, w, b, offs, out):
         with nc.allow_non_contiguous_dma(reason="one bias value a partition"):
             nc.sync.dma_start(bias[:], b.rearrange("(c p) -> p c", p=P))
 
-        def round_w(a, n, copy):
+        def round_w(a, n, copies):
             grouped = sb.tile([P, P * PACK], BF16, name="w_bf_%d_%d" % (a, n), align_bytes=64)
-            copy(
-                grouped[:].rearrange("p (c i t) -> p c t i", i=4, t=PACK),
-                w_raw[a][n].rearrange("p t (c i) -> p c t i", i=4),
-            )
+            width = P // len(copies)
+            for h, copy in enumerate(copies):
+                copy(
+                    grouped[:, h * width * PACK : (h + 1) * width * PACK].rearrange("p (c i t) -> p c t i", i=4, t=PACK),
+                    w_raw[a][n][:, :, h * width : (h + 1) * width].rearrange("p t (c i) -> p c t i", i=4),
+                )
             return grouped
 
         def quantise(a, n):
@@ -116,7 +118,7 @@ def tile_list_tabbag_bias_kernel(tc, tab, w, b, offs, out):
         picked = {}
         acc = [[ps.tile([P, S], F32, name="acc_%d" % n)] for n in range(3)]
         acc.append([ps.tile([P, S // 2], F32, name="acc_3_%d" % h) for h in range(2)])
-        grouped = [[round_w(a, n, nc.scalar.copy) for n in range(M // P - a)] for a in range(2)]
+        grouped = [[round_w(a, n, [nc.scalar.copy]) for n in range(M // P - 2 * a)] for a in range(2)]
 
         quantise(0, 0)
         for g in (0, 2):
@@ -130,14 +132,15 @@ def tile_list_tabbag_bias_kernel(tc, tab, w, b, offs, out):
         for part in range(2):
             multiply(0, 3, range(G), part)
         gather_words(1, 2, 1, "w_raw_0_3")
-        for n in range(2):
-            quantise(1, n)
-            multiply(1, n, range(3))
-        gather_words(1, 3, 1, "w_raw_1_1")
-        for n in range(2):
-            multiply(1, n, [3])
+        quantise(1, 0)
+        multiply(1, 0, range(3))
+        gather_words(1, 3, 1, "w_raw_1_0")
+        multiply(1, 0, [3])
+        quantise(1, 1)
+        multiply(1, 1, range(G))
+        grouped[1].append(round_w(1, 2, [nc.scalar.copy, nc.vector.tensor_copy]))
         quantise(1, 2)
-        grouped[1].append(round_w(1, 3, nc.vector.tensor_copy))
+        grouped[1].append(round_w(1, 3, [nc.vector.tensor_copy]))
         quantise(1, 3)
         early = sb.tile([P, 2, S], F32, name="early", align_bytes=64)
         for n in range(2):

@@ -59,9 +59,9 @@ def tile_list_tabbag_bias_kernel(tc, tab, w, b, offs, out):
         w_raw = [load_w(0, 0, 1), []]
         load_scales()
         tab_words = [load_words(0)]
-        w_raw[0].extend(load_w(0, 1, 2))
+        w_raw[0].extend(load_w(0, 2, 2))
         tab_words.append(load_words(1))
-        w_raw[0].extend(load_w(0, 3, 1))
+        w_raw[0][1:1] = load_w(0, 1, 1)
         for n in range(M // P):
             w_raw[1].extend(load_w(1, n, 1))
         bias = sb.tile([P, M // P], F32, name="bias")
@@ -118,29 +118,29 @@ def tile_list_tabbag_bias_kernel(tc, tab, w, b, offs, out):
         picked = {}
         acc = [[ps.tile([P, S], F32, name="acc_%d" % n)] for n in range(3)]
         acc.append([ps.tile([P, S // 2], F32, name="acc_3_%d" % h) for h in range(2)])
-        grouped = [[round_w(a, n, [nc.scalar.copy]) for n in range(M // P - 2 * a)] for a in range(2)]
+        grouped = [{n: round_w(0, n, [nc.scalar.copy]) for n in (0, 2, 3, 1)}]
+        grouped.append([round_w(1, n, [nc.scalar.copy]) for n in range(2)])
 
         quantise(0, 0)
         for g in (0, 2):
             gather_words(0, g, 2, "picked_0_%d" % g)
             multiply(0, 0, (g, g + 1))
-        for n in (1, 2):
+        for n in (2, 3):
             quantise(0, n)
-            multiply(0, n, range(G))
-        gather_words(1, 0, 2, "picked_1_0")
-        quantise(0, 3)
-        for part in range(2):
-            multiply(0, 3, range(G), part)
-        gather_words(1, 2, 1, "w_raw_0_3")
+            for part in range(len(acc[n])):
+                multiply(0, n, range(G), part)
+        gather_words(1, 0, 3, "picked_1_0")
+        quantise(0, 1)
+        multiply(0, 1, range(G))
         quantise(1, 0)
         multiply(1, 0, range(3))
         gather_words(1, 3, 1, "w_raw_1_0")
         multiply(1, 0, [3])
         quantise(1, 1)
         multiply(1, 1, range(G))
-        grouped[1].append(round_w(1, 2, [nc.scalar.copy, nc.vector.tensor_copy]))
+        grouped[1].append(round_w(1, 2, [nc.scalar.copy]))
+        grouped[1].append(round_w(1, 3, [nc.scalar.copy, nc.vector.tensor_copy]))
         quantise(1, 2)
-        grouped[1].append(round_w(1, 3, [nc.vector.tensor_copy]))
         quantise(1, 3)
         early = sb.tile([P, 2, S], F32, name="early", align_bytes=64)
         for n in range(2):

@@ -32,7 +32,7 @@ def tile_list_tabbag_bias_kernel(tc, tab, w, b, offs, out):
         nc.vector.memset(tab_scales[:].bitcast(I32), 0)
 
         def load_w(a, n, tiles):
-            raw = sb.tile([P, PACK, tiles * P], F32, name="w_raw_%d_%d" % (a, n), align_bytes=64)
+            raw = sb.tile([P, PACK, tiles * P], F32, name="w_raw_%d_%d" % (a, n), align_bytes=256)
             rows = w[a * K_PASS : (a + 1) * K_PASS, n * P : (n + tiles) * P]
             nc.sync.dma_start(raw[:], rows.rearrange("(p j) n -> p j n", j=PACK))
             return [raw[:, :, u * P : (u + 1) * P] for u in range(tiles)]
@@ -79,13 +79,13 @@ def tile_list_tabbag_bias_kernel(tc, tab, w, b, offs, out):
             return grouped
 
         def quantise(a, n):
-            codes = sb.tile([P, P], U32, name="w_codes_%d_%d" % (a, n), align_bytes=64)
-            scales = sb.tile([P, P], U8, name="w_scales_%d_%d" % (a, n), align_bytes=64)
+            codes = sb.tile([P, P], U32, name="w_codes_%d_%d" % (a, n), align_bytes=256)
+            scales = sb.tile([P, P], U8, name="w_scales_%d_%d" % (a, n), align_bytes=256)
             nc.vector.quantize_mx(out=codes[:].bitcast(FP8X4), scales=scales[:], in_=grouped[a][n][:])
             quantised[a, n] = (codes, scales)
 
         def gather_words(a, g, bags, tag):
-            tile = sb.tile([P, bags * S], U32, name="picked_%d_%d" % (a, g), tag=tag, align_bytes=64)
+            tile = sb.tile([P, bags * S], U32, name="picked_%d_%d" % (a, g), tag=tag, align_bytes=256)
             window = tab_words[a][:].bitcast(U32)
             nc.vector.tensor_copy(tile[:], window.indirect(offsets[:, g * LIST_COLS : (g + bags) * LIST_COLS]))
             for u in range(bags):
@@ -111,7 +111,7 @@ def tile_list_tabbag_bias_kernel(tc, tab, w, b, offs, out):
         def finish_on_vector(result, n, part=0):
             nc.vector.tensor_scalar(result, acc[n][part][:], bias[:, n : n + 1], None, mybir.AluOpType.add)
 
-        picked_scales = sb.tile([P, G * S], U8, name="picked_scales", align_bytes=64)
+        picked_scales = sb.tile([P, G * S], U8, name="picked_scales", align_bytes=256)
         nc.vector.tensor_copy(picked_scales[:], tab_scales[:].indirect(offsets[:]))
 
         quantised = {}

@@ -68,13 +68,13 @@ def tile_list_tabbag_bias_kernel(tc, tab, w, b, offs, out):
         with nc.allow_non_contiguous_dma(reason="one bias value a partition"):
             nc.sync.dma_start(bias[:], b.rearrange("(c p) -> p c", p=P))
 
-        def round_w(a, n, copies):
+        def round_w(a, n, copies, scalar_cols=P // 2):
             grouped = sb.tile([P, P * PACK], BF16, name="w_bf_%d_%d" % (a, n), align_bytes=64)
-            width = P // len(copies)
+            cuts = [0, scalar_cols, P][: len(copies)] + [P]
             for h, copy in enumerate(copies):
                 copy(
-                    grouped[:, h * width * PACK : (h + 1) * width * PACK].rearrange("p (c i t) -> p c t i", i=4, t=PACK),
-                    w_raw[a][n][:, :, h * width : (h + 1) * width].rearrange("p t (c i) -> p c t i", i=4),
+                    grouped[:, cuts[h] * PACK : cuts[h + 1] * PACK].rearrange("p (c i t) -> p c t i", i=4, t=PACK),
+                    w_raw[a][n][:, :, cuts[h] : cuts[h + 1]].rearrange("p t (c i) -> p c t i", i=4),
                 )
             return grouped
 
@@ -138,7 +138,7 @@ def tile_list_tabbag_bias_kernel(tc, tab, w, b, offs, out):
         multiply(1, 0, [3])
         quantise(1, 1)
         multiply(1, 1, range(G))
-        grouped[1].append(round_w(1, 2, [nc.scalar.copy]))
+        grouped[1].append(round_w(1, 2, [nc.scalar.copy, nc.vector.tensor_copy], 3 * P // 4))
         grouped[1].append(round_w(1, 3, [nc.scalar.copy, nc.vector.tensor_copy]))
         quantise(1, 2)
         quantise(1, 3)

@@ -78,6 +78,9 @@ def tile_list_tabbag_bias_kernel(tc, tab, w, b, offs, out):
                 )
             return grouped
 
+        def round_on_gpsimd(dst, src):
+            nc.gpsimd.tensor_scalar(dst, src, 1.0, 0.0, mybir.AluOpType.mult, mybir.AluOpType.add)
+
         def quantise(a, n):
             codes = sb.tile([P, P], U32, name="w_codes_%d_%d" % (a, n), align_bytes=256)
             scales = sb.tile([P, P], U8, name="w_scales_%d_%d" % (a, n), align_bytes=256)
@@ -118,8 +121,9 @@ def tile_list_tabbag_bias_kernel(tc, tab, w, b, offs, out):
         picked = {}
         acc = [[ps.tile([P, S], F32, name="acc_%d" % n)] for n in range(3)]
         acc.append([ps.tile([P, S // 2], F32, name="acc_3_%d" % h) for h in range(2)])
-        grouped = [{n: round_w(0, n, [nc.scalar.copy]) for n in (0, 2, 3, 1)}]
-        grouped.append([round_w(1, n, [nc.scalar.copy]) for n in range(2)])
+        grouped = [{n: round_w(0, n, [nc.scalar.copy]) for n in (0, 2, 3)}]
+        grouped[0][1] = round_w(0, 1, [nc.scalar.copy, round_on_gpsimd], 5 * P // 8)
+        grouped.append([round_w(1, n, [nc.scalar.copy, round_on_gpsimd], 5 * P // 8) for n in range(2)])
 
         quantise(0, 0)
         for g in (0, 2):
@@ -129,9 +133,10 @@ def tile_list_tabbag_bias_kernel(tc, tab, w, b, offs, out):
             quantise(0, n)
             for part in range(len(acc[n])):
                 multiply(0, n, range(G), part)
-        gather_words(1, 0, 3, "picked_1_0")
+        gather_words(1, 0, 2, "picked_1_0")
         quantise(0, 1)
         multiply(0, 1, range(G))
+        gather_words(1, 2, 1, "w_raw_0_1")
         quantise(1, 0)
         multiply(1, 0, range(3))
         gather_words(1, 3, 1, "w_raw_1_0")

@@ -87,26 +87,31 @@ def tile_list_tabbag_bias_kernel(tc, tab, w, b, offs, out):
             nc.vector.quantize_mx(out=codes[:].bitcast(FP8X4), scales=scales[:], in_=grouped[a][n][:])
             quantised[a, n] = (codes, scales)
 
-        def gather_words(a, g, bags, tag):
-            tile = sb.tile([P, bags * S], U32, name="picked_%d_%d" % (a, g), tag=tag, align_bytes=256)
+        def gather_words(a, first, count, tag):
+            tile = sb.tile([P, count * P], U32, name="picked_%d_%d" % (a, first), tag=tag, align_bytes=256)
             window = tab_words[a][:].bitcast(U32)
-            nc.vector.tensor_copy(tile[:], window.indirect(offsets[:, g * LIST_COLS : (g + bags) * LIST_COLS]))
-            for u in range(bags):
-                picked[a, g + u] = tile[:, u * S : (u + 1) * S]
+            nc.vector.tensor_copy(tile[:], window.indirect(offsets[:, first * P // 16 : (first + count) * P // 16]))
+            for u in range(count):
+                picked[a, first + u] = (tile, u * P)
 
-        def multiply(a, n, bags, part=0):
+        def multiply(a, n, first, count, last=False):
             codes, scales = quantised[a, n]
-            width = S // len(acc[n])
+            tile, lo = picked[a, first]
+            col = (first % 2) * P
+            bank = acc[n][0][:, col : col + count * P] if len(acc[n]) == 1 else acc[n][first % 2][:]
+            nc.tensor.matmul_mx(
+                out=bank,
+                lhsT=codes[:].bitcast(FP8X4),
+                lhsT_scale=scales[:],
+                rhs=tile[:, lo : lo + count * P].bitcast(FP8X4),
+                rhs_scale=picked_scales[4 * a : P, first * P : (first + count) * P],
+                start=(a == 0 and first < len(acc[n])),
+                stop=last,
+            )
+
+        def multiply_bags(a, n, bags):
             for g in bags:
-                nc.tensor.matmul_mx(
-                    out=acc[n][part][:],
-                    lhsT=codes[:].bitcast(FP8X4),
-                    lhsT_scale=scales[:],
-                    rhs=picked[a, g][:, part * width : (part + 1) * width].bitcast(FP8X4),
-                    rhs_scale=picked_scales[4 * a : P, g * S + part * width : g * S + (part + 1) * width],
-                    start=(a == 0 and g == 0),
-                    stop=(a == 1 and g == G - 1),
-                )
+                multiply(a, n, 2 * g, 2)
 
         def finish_on_scalar(result, n, part=0):
             nc.scalar.activation(result, acc[n][part][:], mybir.ActivationFunctionType.Identity, bias=bias[:, n : n + 1])
@@ -122,41 +127,49 @@ def tile_list_tabbag_bias_kernel(tc, tab, w, b, offs, out):
         acc = [[ps.tile([P, S], F32, name="acc_%d" % n)] for n in range(3)]
         acc.append([ps.tile([P, S // 2], F32, name="acc_3_%d" % h) for h in range(2)])
         grouped = [{n: round_w(0, n, [nc.scalar.copy]) for n in (0, 2, 3)}]
-        grouped[0][1] = round_w(0, 1, [nc.scalar.copy, round_on_gpsimd], 5 * P // 8)
-        grouped.append([round_w(1, n, [nc.scalar.copy, round_on_gpsimd], 5 * P // 8) for n in range(2)])
+        grouped[0][1] = round_w(0, 1, [nc.scalar.copy, round_on_gpsimd], 3 * P // 4)
+        grouped.append([round_w(1, n, [nc.scalar.copy, round_on_gpsimd], 3 * P // 4) for n in range(3)])
 
         quantise(0, 0)
         for g in (0, 2):
-            gather_words(0, g, 2, "picked_0_%d" % g)
-            multiply(0, 0, (g, g + 1))
-        for n in (2, 3):
-            quantise(0, n)
-            for part in range(len(acc[n])):
-                multiply(0, n, range(G), part)
-        gather_words(1, 0, 2, "picked_1_0")
+            gather_words(0, 2 * g, 4, "picked_0_%d" % g)
+            multiply_bags(0, 0, (g, g + 1))
+        quantise(0, 2)
+        multiply_bags(0, 2, range(G))
+        quantise(0, 3)
+        for part in range(2):
+            for g in range(G):
+                multiply(0, 3, 2 * g + part, 1)
+        gather_words(1, 0, 4, "picked_1_0")
         quantise(0, 1)
-        multiply(0, 1, range(G))
-        gather_words(1, 2, 1, "w_raw_0_1")
+        multiply_bags(0, 1, range(G))
+        gather_words(1, 4, 2, "w_raw_0_1")
         quantise(1, 0)
-        multiply(1, 0, range(3))
-        gather_words(1, 3, 1, "w_raw_1_0")
-        multiply(1, 0, [3])
+        multiply_bags(1, 0, range(3))
+        gather_words(1, 6, 1, "w_raw_1_0")
+        multiply(1, 0, 6, 1)
         quantise(1, 1)
-        multiply(1, 1, range(G))
-        grouped[1].append(round_w(1, 2, [nc.scalar.copy, nc.vector.tensor_copy], 3 * P // 4))
-        grouped[1].append(round_w(1, 3, [nc.scalar.copy, nc.vector.tensor_copy]))
+        multiply_bags(1, 1, range(3))
+        multiply(1, 1, 6, 1)
+        gather_words(1, 7, 1, "w_raw_1_1")
+        for n in range(2):
+            multiply(1, n, 7, 1, last=True)
         quantise(1, 2)
+        grouped[1].append(round_w(1, 3, [nc.scalar.copy, nc.vector.tensor_copy]))
         quantise(1, 3)
         early = sb.tile([P, 2, S], F32, name="early", align_bytes=64)
         for n in range(2):
             finish_on_scalar(early[:, n, :], n)
             nc.sync.dma_start(out[n * P : (n + 1) * P, :], early[:, n, :])
-        multiply(1, 2, range(G))
+        multiply_bags(1, 2, range(3))
+        multiply(1, 2, 6, 1)
+        multiply(1, 2, 7, 1, last=True)
         result = sb.tile([P, S], F32, name="result_2")
         finish_on_vector(result[:], 2)
         nc.sync.dma_start(out[2 * P : 3 * P, :], result[:])
         for part, finish in enumerate((finish_on_scalar, finish_on_vector)):
-            multiply(1, 3, range(G), part)
+            for g in range(G):
+                multiply(1, 3, 2 * g + part, 1, last=(g == G - 1))
             result = sb.tile([P, S // 2], F32, name="result_3_%d" % part)
             finish(result[:], 3, part)
             nc.sync.dma_start(out[3 * P : 4 * P, part * (S // 2) : (part + 1) * (S // 2)], result[:])

@@ -78,9 +78,6 @@ def tile_list_tabbag_bias_kernel(tc, tab, w, b, offs, out):
                 )
             return grouped
 
-        def round_on_gpsimd(dst, src):
-            nc.gpsimd.tensor_scalar(dst, src, 1.0, 0.0, mybir.AluOpType.mult, mybir.AluOpType.add)
-
         def quantise(a, n):
             codes = sb.tile([P, P], U32, name="w_codes_%d_%d" % (a, n), align_bytes=256)
             scales = sb.tile([P, P], U8, name="w_scales_%d_%d" % (a, n), align_bytes=256)
@@ -126,9 +123,8 @@ def tile_list_tabbag_bias_kernel(tc, tab, w, b, offs, out):
         picked = {}
         acc = [[ps.tile([P, S], F32, name="acc_%d" % n)] for n in range(3)]
         acc.append([ps.tile([P, S // 2], F32, name="acc_3_%d" % h) for h in range(2)])
-        grouped = [{n: round_w(0, n, [nc.scalar.copy]) for n in (0, 2, 3)}]
-        grouped[0][1] = round_w(0, 1, [nc.scalar.copy, round_on_gpsimd], 3 * P // 4)
-        grouped.append([round_w(1, n, [nc.scalar.copy, round_on_gpsimd], 3 * P // 4) for n in range(3)])
+        grouped = [{n: round_w(0, n, [nc.scalar.copy]) for n in (0, 2, 3, 1)}]
+        grouped.append([round_w(1, n, [nc.scalar.copy]) for n in range(3)])
 
         quantise(0, 0)
         for g in (0, 2):

@@ -110,6 +110,19 @@ def tile_list_tabbag_bias_kernel(tc, tab, w, b, offs, out):
             for g in bags:
                 multiply(a, n, 2 * g, 2)
 
+        def warm_up():
+            codes, scales = quantised[0, 0]
+            for step in range(4):
+                nc.tensor.matmul_mx(
+                    out=first_bank[:, S : S + P],
+                    lhsT=codes[:].bitcast(FP8X4),
+                    lhsT_scale=scales[:],
+                    rhs=codes[:].bitcast(FP8X4),
+                    rhs_scale=scales[:],
+                    start=False,
+                    stop=False,
+                )
+
         def finish_on_scalar(result, n, part=0):
             nc.scalar.activation(result, acc[n][part][:], mybir.ActivationFunctionType.Identity, bias=bias[:, n : n + 1])
 
@@ -121,7 +134,8 @@ def tile_list_tabbag_bias_kernel(tc, tab, w, b, offs, out):
 
         quantised = {}
         picked = {}
-        acc = [[ps.tile([P, S], F32, name="acc_%d" % n)] for n in range(3)]
+        first_bank = ps.tile([P, 2 * S], F32, name="acc_0")
+        acc = [[first_bank[:, 0:S]]] + [[ps.tile([P, S], F32, name="acc_%d" % n)] for n in (1, 2)]
         acc.append([ps.tile([P, S // 2], F32, name="acc_3_%d" % h) for h in range(2)])
         grouped = [{n: round_w(0, n, [nc.scalar.copy]) for n in (0, 2, 3, 1)}]
         grouped.append([round_w(1, n, [nc.scalar.copy]) for n in range(3)])
@@ -130,6 +144,8 @@ def tile_list_tabbag_bias_kernel(tc, tab, w, b, offs, out):
         for g in (0, 2):
             gather_words(0, 2 * g, 4, "picked_0_%d" % g)
             multiply_bags(0, 0, (g, g + 1))
+            if g == 0:
+                warm_up()
         quantise(0, 2)
         multiply_bags(0, 2, range(G))
         quantise(0, 3)

from contextlib import ExitStack

import concourse.mybir as mybir

G, K, M, T, S = 4, 1024, 512, 2048, 256
FLOPS = 2 * G * K * M * S

F32 = mybir.dt.float32
BF16 = mybir.dt.bfloat16
I32 = mybir.dt.int32
U32 = mybir.dt.uint32
U16 = mybir.dt.uint16
U8 = mybir.dt.uint8
FP8X4 = mybir.dt.float8_e4m3fn_x4

P = 128
PACK = 4
K_PASS = P * PACK
HALF = M // 2
LIST_COLS = S // 16


def tile_list_tabbag_bias_kernel(tc, tab, w, b, offs, out):
    nc = tc.nc
    with ExitStack() as ctx:
        sb = ctx.enter_context(tc.tile_pool(name="sb", bufs=1))
        ps = ctx.enter_context(tc.psum_pool(name="ps", bufs=1))

        offsets = sb.tile([P, G * LIST_COLS], U16, name="offsets")

        tab_scales = sb.tile([P, T], U8, name="tab_scales", align_bytes=64)
        nc.vector.memset(tab_scales[:].bitcast(I32), 0)

        def load_w(a, n, tiles):
            raw = sb.tile([P, PACK, tiles * P], F32, name="w_raw_%d_%d" % (a, n), align_bytes=256)
            rows = w[a * K_PASS : (a + 1) * K_PASS, n * P : (n + tiles) * P]
            nc.sync.dma_start(raw[:], rows.rearrange("(p j) n -> p j n", j=PACK))
            return [raw[:, :, u * P : (u + 1) * P] for u in range(tiles)]

        def load_words(a):
            words = sb.tile([P, T], I32, name="tab_words_%d" % a, align_bytes=64)
            src = tab[a, 0 : K_PASS * T].rearrange("(p c) -> p c", p=P).bitcast(I32)
            nc.sync.dma_start(words[:], src)
            return words

        def load_scales():
            for q in (1, 3):
                lo = K_PASS * T + 4 * q * T
                src = tab[:, lo : lo + 4 * T].rearrange("a (r t) -> a r t", r=4).bitcast(I32)
                nc.scalar.dma_start(tab_scales[32 * q : 32 * q + 8, :].bitcast(I32), src)
            for q in (2, 0):
                for a in range(2):
                    lo = K_PASS * T + 4 * q * T
                    src = tab[a, lo : lo + 4 * T].rearrange("(r t) -> r t", r=4).bitcast(I32)
                    first = 32 * q + 4 * a
                    nc.sync.dma_start(tab_scales[first : first + 4, :].bitcast(I32), src)

        nc.sync.dma_start(offsets[:], offs)
        w_raw = [load_w(0, 0, 1), []]
        load_scales()
        tab_words = [load_words(0)]
        w_raw[0].extend(load_w(0, 2, 2))
        tab_words.append(load_words(1))
        w_raw[0][1:1] = load_w(0, 1, 1)
        for n in range(M // P):
            w_raw[1].extend(load_w(1, n, 1))
        bias = sb.tile([P, M // P], F32, name="bias")
        with nc.allow_non_contiguous_dma(reason="one bias value a partition"):
            nc.sync.dma_start(bias[:], b.rearrange("(c p) -> p c", p=P))

        def round_w(a, n, copies, scalar_cols=P // 2):
            grouped = sb.tile([P, P * PACK], BF16, name="w_bf_%d_%d" % (a, n), align_bytes=64)
            cuts = [0, scalar_cols, P][: len(copies)] + [P]
            for h, copy in enumerate(copies):
                copy(
                    grouped[:, cuts[h] * PACK : cuts[h + 1] * PACK].rearrange("p (c i t) -> p c t i", i=4, t=PACK),
                    w_raw[a][n][:, :, cuts[h] : cuts[h + 1]].rearrange("p t (c i) -> p c t i", i=4),
                )
            return grouped

        def quantise(a, n):
            codes = sb.tile([P, P], U32, name="w_codes_%d_%d" % (a, n), align_bytes=256)
            scales = sb.tile([P, P], U8, name="w_scales_%d_%d" % (a, n), align_bytes=256)
            nc.vector.quantize_mx(out=codes[:].bitcast(FP8X4), scales=scales[:], in_=grouped[a][n][:])
            quantised[a, n] = (codes, scales)

        def gather_words(a, first, count, tag):
            tile = sb.tile([P, count * P], U32, name="picked_%d_%d" % (a, first), tag=tag, align_bytes=256)
            window = tab_words[a][:].bitcast(U32)
            nc.vector.tensor_copy(tile[:], window.indirect(offsets[:, first * P // 16 : (first + count) * P // 16]))
            for u in range(count):
                picked[a, first + u] = (tile, u * P)

        def multiply(a, n, first, count, last=False):
            codes, scales = quantised[a, n]
            tile, lo = picked[a, first]
            col = (first % 2) * P
            bank = acc[n][0][:, col : col + count * P] if len(acc[n]) == 1 else acc[n][first % 2][:]
            nc.tensor.matmul_mx(
                out=bank,
                lhsT=codes[:].bitcast(FP8X4),
                lhsT_scale=scales[:],
                rhs=tile[:, lo : lo + count * P].bitcast(FP8X4),
                rhs_scale=picked_scales[4 * a : P, first * P : (first + count) * P],
                start=(a == 0 and first < len(acc[n])),
                stop=last,
            )

        def multiply_bags(a, n, bags):
            for g in bags:
                multiply(a, n, 2 * g, 2)

        def warm_up():
            codes, scales = quantised[0, 0]
            for step in range(4):
                nc.tensor.matmul_mx(
                    out=first_bank[:, S : S + P],
                    lhsT=codes[:].bitcast(FP8X4),
                    lhsT_scale=scales[:],
                    rhs=codes[:].bitcast(FP8X4),
                    rhs_scale=scales[:],
                    start=False,
                    stop=False,
                )

        def finish_on_scalar(result, n, part=0):
            nc.scalar.activation(result, acc[n][part][:], mybir.ActivationFunctionType.Identity, bias=bias[:, n : n + 1])

        def finish_on_vector(result, n, part=0):
            nc.vector.tensor_scalar(result, acc[n][part][:], bias[:, n : n + 1], None, mybir.AluOpType.add)

        picked_scales = sb.tile([P, G * S], U8, name="picked_scales", align_bytes=256)
        nc.vector.tensor_copy(picked_scales[:], tab_scales[:].indirect(offsets[:]))

        quantised = {}
        picked = {}
        first_bank = ps.tile([P, 2 * S], F32, name="acc_0")
        acc = [[first_bank[:, 0:S]]] + [[ps.tile([P, S], F32, name="acc_%d" % n)] for n in (1, 2)]
        acc.append([ps.tile([P, S // 2], F32, name="acc_3_%d" % h) for h in range(2)])
        grouped = [{n: round_w(0, n, [nc.scalar.copy]) for n in (0, 2, 3, 1)}]
        grouped.append([round_w(1, n, [nc.scalar.copy]) for n in range(3)])

        quantise(0, 0)
        for g in (0, 2):
            gather_words(0, 2 * g, 4, "picked_0_%d" % g)
            multiply_bags(0, 0, (g, g + 1))
            if g == 0:
                warm_up()
        quantise(0, 2)
        multiply_bags(0, 2, range(G))
        quantise(0, 3)
        for part in range(2):
            for g in range(G):
                multiply(0, 3, 2 * g + part, 1)
        gather_words(1, 0, 4, "picked_1_0")
        quantise(0, 1)
        multiply_bags(0, 1, range(G))
        gather_words(1, 4, 2, "w_raw_0_1")
        quantise(1, 0)
        multiply_bags(1, 0, range(3))
        gather_words(1, 6, 1, "w_raw_1_0")
        multiply(1, 0, 6, 1)
        quantise(1, 1)
        multiply_bags(1, 1, range(3))
        multiply(1, 1, 6, 1)
        gather_words(1, 7, 1, "w_raw_1_1")
        for n in range(2):
            multiply(1, n, 7, 1, last=True)
        quantise(1, 2)
        grouped[1].append(round_w(1, 3, [nc.scalar.copy, nc.vector.tensor_copy]))
        quantise(1, 3)
        early = sb.tile([P, 2, S], F32, name="early", align_bytes=64)
        for n in range(2):
            finish_on_scalar(early[:, n, :], n)
            nc.sync.dma_start(out[n * P : (n + 1) * P, :], early[:, n, :])
        multiply_bags(1, 2, range(3))
        multiply(1, 2, 6, 1)
        multiply(1, 2, 7, 1, last=True)
        result = sb.tile([P, S], F32, name="result_2")
        finish_on_vector(result[:], 2)
        nc.sync.dma_start(out[2 * P : 3 * P, :], result[:])
        for part, finish in enumerate((finish_on_scalar, finish_on_vector)):
            for g in range(G):
                multiply(1, 3, 2 * g + part, 1, last=(g == G - 1))
            result = sb.tile([P, S // 2], F32, name="result_3_%d" % part)
            finish(result[:], 3, part)
            nc.sync.dma_start(out[3 * P : 4 * P, part * (S // 2) : (part + 1) * (S // 2)], result[:])
